import numpy as np, ml_dtypes
CORES = [35,38,43,46]
N = 4
import mx_ref
BF = ml_dtypes.bfloat16
def entries(a):
    return np.ascontiguousarray(a.T).reshape(-1)
def table(e):
    return np.ascontiguousarray(np.reshape(e, (-1, 16)).T).astype(np.int32)
def cols(t, e):
    v = np.concatenate([t.reshape(128, -1, 4), np.zeros((128, 1, 4), BF)], axis=1)
    return np.ascontiguousarray(v[:, e]).reshape(128, -1)
def tile(rs):
    return np.stack(rs, axis=2).reshape(128, -1).astype(BF)
def cut(t, i, w=512):
    return t[:, w * i:w * i + w]
def rowtile(v, k):
    z = np.concatenate([v, np.zeros((1, v.shape[1]), BF)])
    return np.concatenate([np.ascontiguousarray(z[k[:, 4 * m:4 * m + 4]].transpose(0, 2, 1)).reshape(128, -1) for m in range(k.shape[1] // 4)], axis=1)
def f(rng, *shape):
    return mx_ref.flush((rng.standard_normal(shape, dtype=np.float32) * np.exp2(rng.integers(-2, 3, shape[:-1] + (1,)))).astype(BF))
def wide(rng, *shape, cols=0):
    v = rng.standard_normal(shape, dtype=np.float32) * np.exp2(rng.integers(-12, 13, shape)).astype(np.float32)
    if cols: v *= np.repeat(np.exp2(rng.integers(-cols, cols + 1, shape[:-2] + (1, shape[-1] // 4))) * (rng.random(shape[:-2] + (1, shape[-1] // 4)) > 0.0625), 4, axis=-1).astype(np.float32)
    return mx_ref.flush(v.astype(BF))
T, HU, ACT = 512, 1024, 512
def lists(rng, how=None):
    a = []
    for r in range(N):
        e = rng.permutation(HU)[:ACT]
        if how == "reversed": e = np.sort(e)[::-1]
        if how == "clustered": e = rng.integers(0, HU - ACT + 1) + np.arange(ACT)
        a.append(e)
    return {"act": np.stack([e.reshape(128, 4).astype(np.int32) for e in a]), "actc": np.stack([table(e) for e in a])}
def setup_inputs(rng):
    return {"x": f(rng, N, 128, 4 * T), "w1": f(rng, N, 128, 4 * HU), "w2": f(rng, N, HU, 512), **lists(rng)}
def setup_inputs_clustered(rng):
    return {**setup_inputs(rng), **lists(rng, "clustered")}
def setup_inputs_dead(rng):
    d = setup_inputs(rng); d["x"] = np.abs(d["x"])
    for r in range(N):
        k = d["act"][r].reshape(-1)[rng.permutation(ACT)[:ACT // 2]]
        w = d["w1"][r].reshape(128, HU, 4)
        w[:, k] = -np.abs(w[:, k])
        d["w1"][r] = w.reshape(128, -1)
    return d
def setup_inputs_giant(rng):
    d = setup_inputs(rng)
    for r in range(N):
        k = d["act"][r].reshape(-1)[rng.permutation(ACT)[:ACT // 32]]
        d["w2"][r, k] = (d["w2"][r, k].astype(np.float32) * np.float32(4096)).astype(BF)
    return d
def setup_inputs_reversed(rng):
    return {**setup_inputs(rng), **lists(rng, "reversed")}
def setup_inputs_spread(rng):
    d = setup_inputs(rng); d["x"] = wide(rng, N, 128, 4 * T); d["w2"] = wide(rng, N, HU, 512); return d
def check_inputs(d):
    b = []
    for r in range(N):
        e = d["act"][r].reshape(-1)
        if e.min() < 0 or e.max() >= HU or len(set(e.tolist())) != ACT: b.append("act")
        if (entries(d["actc"][r]) != e).any(): b.append("actc")
    return b
def reference(x, w1, w2, act, actc):
    y = np.zeros((N, 128, 4 * T), np.float32)
    X = [mx_ref.quantize(x[r]) for r in range(N)]
    for s in range(N):
        A = [mx_ref.quantize(cols(w1[s], act[s][:, b])) for b in range(4)]
        rows = rowtile(w2[s], act[s])
        B = [mx_ref.quantize(np.ascontiguousarray(cut(rows, o))) for o in range(4)]
        for r in range(N):
            H = mx_ref.quantize(tile([np.maximum(mx_ref.matmul(A[b], X[r]), np.float32(0)) * np.float32(0.05) for b in range(4)]))
            for o in range(4): y[r][:, T * o:T * o + T] += mx_ref.matmul(B[o], H)
    return {"y": y}

@@ -1,0 +1,226 @@
+from concourse.bass import DstId, RemoteDMATransfer, IndirectOffsetOnAxis
+from concourse.mybir import dt, AluOpType, ActivationFunctionType
+
+N, C = 4, 512
+W = 4 * C
+SCRATCH = {
+    "lst": ("sbuf", [128, 4], "int32"),
+    "tabs": ("sbuf", [128, 32], "int32"),
+    "quad": ("sbuf", [128, 32], "int32"),
+    "offs": ("sbuf", [128, 128], "uint16"),
+    "w1b": ("sbuf", [128, 4096], "bfloat16"),
+    "xb": ("sbuf", [128, W], "bfloat16"),
+    "ab": ("sbuf", [128, W], "bfloat16"),
+    "w2g": ("sbuf", [128, W], "bfloat16"),
+    "bb": ("sbuf", [128, W], "bfloat16"),
+    "h0": ("sbuf", [128, W], "bfloat16"), "h1": ("sbuf", [128, W], "bfloat16"),
+    "h2": ("sbuf", [128, W], "bfloat16"), "h3": ("sbuf", [128, W], "bfloat16"),
+    "xq": ("sbuf", [128, C], "float8_e4m3fn_x4"), "xp": ("sbuf", [128, C], "uint8"),
+    "aq": ("sbuf", [128, N * C], "float8_e4m3fn_x4"), "ap": ("sbuf", [128, N * C], "uint8"),
+    "bq": ("sbuf", [128, N * C], "float8_e4m3fn_x4"), "bp": ("sbuf", [128, N * C], "uint8"),
+    "hq": ("sbuf", [128, N * C], "float8_e4m3fn_x4"), "hp": ("sbuf", [128, N * C], "uint8"),
+    "yb": ("sbuf", [128, W], "float32"),
+    "zps": ("psum", [128, W], "float32"),
+    "yps": ("psum", [128, W], "float32"),
+}
+SEMAPHORES = (["lact", "ltab", "lw1", "lx", "lxg", "vquad", "vrep", "voff", "gath", "qa", "qx", "qb", "bcs", "bcv", "sent", "stored"]
+              + ["ix%d" % t for t in range(4)]
+              + ["z%d" % b for b in range(4)] + ["e%d" % b for b in range(4)]
+              + ["h%d" % s for s in range(N)]
+              + ["yd%d" % o for o in range(4)] + ["yc%d" % o for o in range(4)]
+              + ["%s%d" % (k, s) for s in range(N) for k in ("ax", "ay", "bx", "by", "bz")])
+
+
+def lanes(core, cores, topo):
+    others = [c for c in cores if c != core]
+    far = [c for c in others if topo.chip(c) != topo.chip(core)]
+    near = [c for c in others if topo.chip(c) == topo.chip(core)]
+    out = sorted({e for c in far for e in topo.engines(core, c)})
+    plan = {}
+    for group, es in ((far, out), (near, [e for c in near[:1] for e in topo.engines(core, c) if e not in out])):
+        for i, c in enumerate(group):
+            k = len(es) // len(group)
+            plan[c] = es[i * k:i * k + k]
+    return plan
+
+
+def rank_program(g, core, T, topo):
+    r = T.rank_of(core)
+    if r is None:
+        return
+    S = T.sem
+    MUL, ADD, MAX = AluOpType.mult, AluOpType.add, AluOpType.max
+    COPY, RELU = ActivationFunctionType.Copy, ActivationFunctionType.Relu
+    cores = list(T.cores)
+    send = lanes(core, cores, topo)
+    recv = {s: lanes(cores[s], cores, topo)[core] for s in range(N) if s != r}
+    near = [s for s in recv if topo.chip(cores[s]) == topo.chip(core)]
+    far = [s for s in recv if s not in near]
+    far.sort(key=lambda s: topo.die(cores[s]) != topo.die(core))
+    order = [r] + near + far
+
+    def q(name, s, a=0, n=C):
+        return T[name][:, C * s + a:C * s + a + n]
+
+    def tab(eng, h, c):
+        eng.dma_start(T.tabs[16 * h:16 * h + 16, 4 * c:4 * c + 4], T.act[16 * c:16 * c + 16, :]).then_inc(S.ltab, 16)
+
+    XG = 256
+    g.sync.dma_start(T.lst[:], T.act[:]).then_inc(S.lact, 16)
+    for c in range(8):
+        tab(g.sync, 0, c)
+        tab(g.scalar, 1, c)
+    g.scalar.dma_start(T.w1b[:], T.w1[:]).then_inc(S.lw1, 16)
+    g.scalar.dma_start(T.xb[:, XG:], T.x[:, XG:]).then_inc(S.lx, 16)
+    g.dma_start(T.xb[:, 0:XG], T.x[:, 0:XG]).then_inc(S.lxg, 16)
+
+    g.wait_ge(S.lact, 16)
+    for t in range(4):
+        g.indirect_dma_start(T.w2g[:, C * t:C * t + C], None, T.w2[:], IndirectOffsetOnAxis(ap=T.lst[:, t:t + 1], axis=0),
+                             bounds_check=1023).then_inc(S["ix%d" % t], 16)
+    total = [0]
+
+    def fused(sem, pieces):
+        k = len(pieces)
+        tr = []
+        for c in cores:
+            if c == core:
+                continue
+            rid, pid, _ = topo.addr(c)
+            n = len(send[c]) // k
+            for i, p in enumerate(pieces):
+                tr.append(RemoteDMATransfer(dst_ids=[DstId(rid=rid, pnc=pid)], dma_engine_mask=sum(1 << e for e in send[c][i * n:i * n + n]),
+                                            remote_sem=S["%s%d" % (sem, r)], src=p, dst=p))
+                total[0] += n
+        g.remote_dma_fused(tr, local_sem=S.sent)
+
+    def codes(name, a, n):
+        return q(name, r, a, n).bitcast(dt.uint8)
+
+    g.wait_ge(S.qa, 1)
+    fused("ax", [q("ap", r), codes("aq", 0, 128)])
+    fused("ay", [codes("aq", 128, 384)])
+    g.wait_ge(S.qb, 4)
+    fused("bx", [q("bp", r), codes("bq", 0, 128)])
+    fused("by", [codes("bq", 128, 128), codes("bq", 256, 128)])
+    fused("bz", [codes("bq", 384, 128)])
+    g.wait_ge(S.sent, total[0])
+
+    v, a = g.vector, g.scalar
+    v.wait_ge(S.ltab, 256)
+    for b in range(4):
+        v.tensor_scalar(T.quad[0:32, 8 * b:8 * b + 8], T.tabs[0:32, b:32:4], 4, None, MUL).then_inc(S.vquad, 1)
+    v.wait_ge(S.vquad, 4)
+    for k in range(1, 4):
+        v.tensor_copy(T.quad[32 * k:32 * k + 32, :], T.quad[0:32, :]).then_inc(S.vrep, 1)
+    v.wait_ge(S.vrep, 3)
+    for t in range(4):
+        v.tensor_scalar(T.offs[:, 32 * t:32 * t + 32], T.quad[:], t, None, ADD).then_inc(S.voff, 1)
+
+    def gather(t):
+        return T.ab[:, t:W:4], T.w1b[:, 0:4096].indirect(T.offs[:, 32 * t:32 * t + 32])
+
+    for e in (v, a):
+        e.wait_ge(S.voff, 4)
+        e.wait_ge(S.lw1, 16)
+    for t in (0, 1):
+        v.tensor_copy(*gather(t)).then_inc(S.gath, 1)
+    for t in (2, 3):
+        a.activation(*gather(t), COPY).then_inc(S.gath, 1)
+    v.wait_ge(S.gath, 4)
+    v.quantize_mx(q("aq", r), q("ap", r), T.ab[:]).then_inc(S.qa, 1)
+    v.wait_ge(S.lx, 16)
+    v.wait_ge(S.lxg, 16)
+    v.quantize_mx(T.xq[:], T.xp[:], T.xb[:]).then_inc(S.qx, 1)
+
+    def relu(i, b, vec):
+        s = order[i]
+        e = v if vec else a
+        out, z = T["h%d" % s][:, b:W:4], T.zps[:, C * b:C * b + C]
+        e.wait_ge(S["z%d" % b], i + 1)
+        if vec:
+            v.tensor_scalar(out, z, 0.0, 0.05, MAX, MUL).then_inc(S["e%d" % b], 1)
+        else:
+            a.activation(out, z, RELU, scale=0.05).then_inc(S["e%d" % b], 1)
+
+    def hidden(i, scal, vect):
+        s = order[i]
+        for b in scal:
+            relu(i, b, False)
+        for b in vect:
+            relu(i, b, True)
+        for b in range(4):
+            v.wait_ge(S["e%d" % b], i + 1)
+        v.quantize_mx(q("hq", s), q("hp", s), T["h%d" % s][:]).then_inc(S["h%d" % s], 1)
+
+    def rows(t):
+        return T.bb[:, t:W:4], T.w2g[:, C * t:C * t + C]
+
+    for t in (0, 1):
+        a.wait_ge(S["ix%d" % t], 16)
+        a.activation(*rows(t), COPY).then_inc(S.bcs, 1)
+    hidden(0, (0, 2), (1, 3))
+    a.wait_ge(S.ix2, 16)
+    a.activation(*rows(2), COPY).then_inc(S.bcs, 1)
+    v.wait_ge(S.ix3, 16)
+    v.tensor_copy(*rows(3)).then_inc(S.bcv, 1)
+    v.wait_ge(S.bcv, 1)
+    v.wait_ge(S.bcs, 3)
+    for o in range(4):
+        v.quantize_mx(q("bq", r, 128 * o, 128), q("bp", r, 128 * o, 128), T.bb[:, C * o:C * o + C]).then_inc(S.qb, 1)
+    hidden(1, (0, 2), (1, 3))
+    hidden(2, (0, 2), (1, 3))
+    hidden(3, (0, 1, 2), (3,))
+    for o in range(4):
+        e = v if o % 2 == 0 else a
+        cols = slice(C * o, C * o + C)
+        e.wait_ge(S["yd%d" % o], 1)
+        if o % 2 == 0:
+            v.tensor_copy(T.yb[:, cols], T.yps[:, cols]).then_inc(S["yc%d" % o], 1)
+        else:
+            a.activation(T.yb[:, cols], T.yps[:, cols], COPY).then_inc(S["yc%d" % o], 1)
+
+    p = g.tensor
+
+    def first(i):
+        s = order[i]
+        if s == r:
+            p.wait_ge(S.qa, 1)
+            p.wait_ge(S.qx, 1)
+        for b in range(4):
+            if s != r and b < 2:
+                p.wait_ge(S["%s%d" % ("ax" if b == 0 else "ay", s)], len(recv[s]))
+            if i:
+                p.wait_ge(S["e%d" % b], i)
+            p.matmul_mx(T.zps[:, C * b:C * b + C], q("aq", s, 128 * b, 128), q("ap", s, 128 * b, 128), T.xq[:], T.xp[:],
+                        True, True).then_inc(S["z%d" % b], 1)
+
+    def second(i, o):
+        s = order[i]
+        if o == 0:
+            p.wait_ge(S["h%d" % s], 1)
+        if s == r:
+            if o == 0:
+                p.wait_ge(S.qb, 4)
+        elif o != 2:
+            p.wait_ge(S["%s%d" % (("bx", "by", None, "bz")[o], s)], len(recv[s]))
+        m = p.matmul_mx(T.yps[:, C * o:C * o + C], q("bq", s, 128 * o, 128), q("bp", s, 128 * o, 128), q("hq", s), q("hp", s),
+                        i == 0, i == N - 1)
+        if i == N - 1:
+            m.then_inc(S["yd%d" % o], 1)
+
+    first(0)
+    first(1)
+    for o in range(4):
+        second(0, o)
+    first(2)
+    first(3)
+    for o in range(4):
+        for i in (1, 2, 3):
+            second(i, o)
+
+    for o in range(4):
+        cols = slice(C * o, C * o + C)
+        g.sync.wait_ge(S["yc%d" % o], 1)
+        g.sync.dma_start(T.y[:, cols], T.yb[:, cols]).then_inc(S.stored, 16)
+    g.sync.wait_ge(S.stored, 64)

@@ -3,32 +3,26 @@ from concourse.mybir import dt, AluOpType, ActivationFunctionType
 
 N, C = 4, 512
 W = 4 * C
+BF, F8 = "bfloat16", "float8_e4m3fn_x4"
 SCRATCH = {
     "lst": ("sbuf", [128, 4], "int32"),
     "tabs": ("sbuf", [128, 32], "int32"),
     "quad": ("sbuf", [128, 32], "int32"),
     "offs": ("sbuf", [128, 128], "uint16"),
-    "w1b": ("sbuf", [128, 4096], "bfloat16"),
-    "xb": ("sbuf", [128, W], "bfloat16"),
-    "ab": ("sbuf", [128, W], "bfloat16"),
-    "w2g": ("sbuf", [128, W], "bfloat16"),
-    "bb": ("sbuf", [128, W], "bfloat16"),
-    "h0": ("sbuf", [128, W], "bfloat16"), "h1": ("sbuf", [128, W], "bfloat16"),
-    "h2": ("sbuf", [128, W], "bfloat16"), "h3": ("sbuf", [128, W], "bfloat16"),
-    "xq": ("sbuf", [128, C], "float8_e4m3fn_x4"), "xp": ("sbuf", [128, C], "uint8"),
-    "aq": ("sbuf", [128, N * C], "float8_e4m3fn_x4"), "ap": ("sbuf", [128, N * C], "uint8"),
-    "bq": ("sbuf", [128, N * C], "float8_e4m3fn_x4"), "bp": ("sbuf", [128, N * C], "uint8"),
-    "hq": ("sbuf", [128, N * C], "float8_e4m3fn_x4"), "hp": ("sbuf", [128, N * C], "uint8"),
+    "w1b": ("sbuf", [128, 4096], BF), "xb": ("sbuf", [128, W], BF), "ab": ("sbuf", [128, W], BF),
+    "w2g": ("sbuf", [128, W], BF), "bb": ("sbuf", [128, W], BF),
+    "h0": ("sbuf", [128, W], BF), "h1": ("sbuf", [128, W], BF), "h2": ("sbuf", [128, W], BF), "h3": ("sbuf", [128, W], BF),
+    "xq": ("sbuf", [128, C], F8), "xp": ("sbuf", [128, C], "uint8"),
+    "aq": ("sbuf", [128, N * C], F8), "ap": ("sbuf", [128, N * C], "uint8"),
+    "bq": ("sbuf", [128, N * C], F8), "bp": ("sbuf", [128, N * C], "uint8"),
+    "hq": ("sbuf", [128, N * C], F8), "hp": ("sbuf", [128, N * C], "uint8"),
     "yb": ("sbuf", [128, W], "float32"),
     "zps": ("psum", [128, W], "float32"),
     "yps": ("psum", [128, W], "float32"),
 }
-SEMAPHORES = (["lact", "ltab", "lw1", "lx", "lxg", "vquad", "vrep", "voff", "gath", "qa", "qx", "qb", "bcs", "bcv", "sent", "stored"]
-              + ["ix%d" % t for t in range(4)]
-              + ["z%d" % b for b in range(4)] + ["e%d" % b for b in range(4)]
-              + ["h%d" % s for s in range(N)]
-              + ["yd%d" % o for o in range(4)] + ["yc%d" % o for o in range(4)]
-              + ["%s%d" % (k, s) for s in range(N) for k in ("ax", "ay", "bx", "by", "bz")])
+SEMAPHORES = (["lact", "ltab", "lw1", "lx", "lxg", "vquad", "vrep", "voff", "gath0", "gath1", "qa0", "qa1", "qx", "qb",
+               "bcs", "bcv", "sent", "stored"]
+              + ["%s%d" % (k, i) for i in range(4) for k in ("ix", "z", "e", "h", "yd", "yc", "ax", "ay", "az", "bx", "by", "bz")])
 
 
 def lanes(core, cores, topo):
@@ -55,8 +49,7 @@ def rank_program(g, core, T, topo):
     send = lanes(core, cores, topo)
     recv = {s: lanes(cores[s], cores, topo)[core] for s in range(N) if s != r}
     near = [s for s in recv if topo.chip(cores[s]) == topo.chip(core)]
-    far = [s for s in recv if s not in near]
-    far.sort(key=lambda s: topo.die(cores[s]) != topo.die(core))
+    far = sorted([s for s in recv if s not in near], key=lambda s: topo.die(cores[s]) != topo.die(core))
     order = [r] + near + far
 
     def q(name, s, a=0, n=C):
@@ -74,36 +67,38 @@ def rank_program(g, core, T, topo):
     g.scalar.dma_start(T.xb[:, XG:], T.x[:, XG:]).then_inc(S.lx, 16)
     g.dma_start(T.xb[:, 0:XG], T.x[:, 0:XG]).then_inc(S.lxg, 16)
 
-    g.wait_ge(S.lact, 16)
-    for t in range(4):
-        g.indirect_dma_start(T.w2g[:, C * t:C * t + C], None, T.w2[:], IndirectOffsetOnAxis(ap=T.lst[:, t:t + 1], axis=0),
-                             bounds_check=1023).then_inc(S["ix%d" % t], 16)
     total = [0]
 
     def fused(sem, pieces):
-        k = len(pieces)
         tr = []
         for c in cores:
             if c == core:
                 continue
             rid, pid, _ = topo.addr(c)
-            n = len(send[c]) // k
+            n = len(send[c]) // len(pieces)
             for i, p in enumerate(pieces):
                 tr.append(RemoteDMATransfer(dst_ids=[DstId(rid=rid, pnc=pid)], dma_engine_mask=sum(1 << e for e in send[c][i * n:i * n + n]),
                                             remote_sem=S["%s%d" % (sem, r)], src=p, dst=p))
                 total[0] += n
         g.remote_dma_fused(tr, local_sem=S.sent)
 
-    def codes(name, a, n):
-        return q(name, r, a, n).bitcast(dt.uint8)
+    def codes(name, b, n=1):
+        return q(name, r, 128 * b, 128 * n).bitcast(dt.uint8)
 
-    g.wait_ge(S.qa, 1)
-    fused("ax", [q("ap", r), codes("aq", 0, 128)])
-    fused("ay", [codes("aq", 128, 384)])
-    g.wait_ge(S.qb, 4)
-    fused("bx", [q("bp", r), codes("bq", 0, 128)])
-    fused("by", [codes("bq", 128, 128), codes("bq", 256, 128)])
-    fused("bz", [codes("bq", 384, 128)])
+    g.wait_ge(S.lact, 16)
+    for t in range(4):
+        if t == 3:
+            g.wait_ge(S.qa0, 1)
+            fused("ax", [codes("aq", 0, 2)])
+        g.indirect_dma_start(T.w2g[:, C * t:C * t + C], None, T.w2[:], IndirectOffsetOnAxis(ap=T.lst[:, t:t + 1], axis=0),
+                             bounds_check=1023).then_inc(S["ix%d" % t], 16)
+    g.wait_ge(S.qa1, 1)
+    fused("ay", [q("ap", r), codes("aq", 2)])
+    fused("az", [codes("aq", 3)])
+    g.wait_ge(S.qb, 1)
+    fused("bx", [q("bp", r), codes("bq", 0)])
+    fused("by", [codes("bq", 1), codes("bq", 2)])
+    fused("bz", [codes("bq", 3)])
     g.wait_ge(S.sent, total[0])
 
     v, a = g.vector, g.scalar
@@ -116,27 +111,28 @@ def rank_program(g, core, T, topo):
     v.wait_ge(S.vrep, 3)
     for t in range(4):
         v.tensor_scalar(T.offs[:, 32 * t:32 * t + 32], T.quad[:], t, None, ADD).then_inc(S.voff, 1)
-
-    def gather(t):
-        return T.ab[:, t:W:4], T.w1b[:, 0:4096].indirect(T.offs[:, 32 * t:32 * t + 32])
-
     for e in (v, a):
         e.wait_ge(S.voff, 4)
         e.wait_ge(S.lw1, 16)
-    for t in (0, 1):
-        v.tensor_copy(*gather(t)).then_inc(S.gath, 1)
-    for t in (2, 3):
-        a.activation(*gather(t), COPY).then_inc(S.gath, 1)
-    v.wait_ge(S.gath, 4)
-    v.quantize_mx(q("aq", r), q("ap", r), T.ab[:]).then_inc(S.qa, 1)
+    for k, (lo, hi) in enumerate(((0, 256), (256, 512))):
+
+        def gather(t):
+            return (T.ab[:, 4 * lo + t:4 * hi:4],
+                    T.w1b[:, 0:4096].indirect(T.offs[:, 32 * t + lo // 16:32 * t + hi // 16]))
+
+        for t in (0, 1):
+            v.tensor_copy(*gather(t)).then_inc(S["gath%d" % k], 1)
+        for t in (2, 3):
+            a.activation(*gather(t), COPY).then_inc(S["gath%d" % k], 1)
+        v.wait_ge(S["gath%d" % k], 4)
+        v.quantize_mx(q("aq", r, lo, hi - lo), q("ap", r, lo, hi - lo), T.ab[:, 4 * lo:4 * hi]).then_inc(S["qa%d" % k], 1)
     v.wait_ge(S.lx, 16)
     v.wait_ge(S.lxg, 16)
     v.quantize_mx(T.xq[:], T.xp[:], T.xb[:]).then_inc(S.qx, 1)
 
     def relu(i, b, vec):
-        s = order[i]
         e = v if vec else a
-        out, z = T["h%d" % s][:, b:W:4], T.zps[:, C * b:C * b + C]
+        out, z = T["h%d" % order[i]][:, b:W:4], T.zps[:, C * b:C * b + C]
         e.wait_ge(S["z%d" % b], i + 1)
         if vec:
             v.tensor_scalar(out, z, 0.0, 0.05, MAX, MUL).then_inc(S["e%d" % b], 1)
@@ -166,15 +162,13 @@ def rank_program(g, core, T, topo):
     v.tensor_copy(*rows(3)).then_inc(S.bcv, 1)
     v.wait_ge(S.bcv, 1)
     v.wait_ge(S.bcs, 3)
-    for o in range(4):
-        v.quantize_mx(q("bq", r, 128 * o, 128), q("bp", r, 128 * o, 128), T.bb[:, C * o:C * o + C]).then_inc(S.qb, 1)
-    hidden(1, (0, 2), (1, 3))
+    v.quantize_mx(q("bq", r), q("bp", r), T.bb[:]).then_inc(S.qb, 1)
+    hidden(1, (0, 1, 2), (3,))
     hidden(2, (0, 2), (1, 3))
     hidden(3, (0, 1, 2), (3,))
     for o in range(4):
-        e = v if o % 2 == 0 else a
         cols = slice(C * o, C * o + C)
-        e.wait_ge(S["yd%d" % o], 1)
+        (a if o % 2 else v).wait_ge(S["yd%d" % o], 1)
         if o % 2 == 0:
             v.tensor_copy(T.yb[:, cols], T.yps[:, cols]).then_inc(S["yc%d" % o], 1)
         else:
@@ -184,12 +178,13 @@ def rank_program(g, core, T, topo):
 
     def first(i):
         s = order[i]
-        if s == r:
-            p.wait_ge(S.qa, 1)
-            p.wait_ge(S.qx, 1)
+        for k in ("qa0", "qa1", "qx") if s == r else ():
+            p.wait_ge(S[k], 1)
+        for k in ("ax", "ay") if s != r else ():
+            p.wait_ge(S["%s%d" % (k, s)], len(recv[s]))
         for b in range(4):
-            if s != r and b < 2:
-                p.wait_ge(S["%s%d" % ("ax" if b == 0 else "ay", s)], len(recv[s]))
+            if s != r and b == 3:
+                p.wait_ge(S["az%d" % s], len(recv[s]))
             if i:
                 p.wait_ge(S["e%d" % b], i)
             p.matmul_mx(T.zps[:, C * b:C * b + C], q("aq", s, 128 * b, 128), q("ap", s, 128 * b, 128), T.xq[:], T.xp[:],
@@ -201,7 +196,7 @@ def rank_program(g, core, T, topo):
             p.wait_ge(S["h%d" % s], 1)
         if s == r:
             if o == 0:
-                p.wait_ge(S.qb, 4)
+                p.wait_ge(S.qb, 1)
         elif o != 2:
             p.wait_ge(S["%s%d" % (("bx", "by", None, "bz")[o], s)], len(recv[s]))
         m = p.matmul_mx(T.yps[:, C * o:C * o + C], q("bq", s, 128 * o, 128), q("bp", s, 128 * o, 128), q("hq", s), q("hp", s),
@@ -211,13 +206,12 @@ def rank_program(g, core, T, topo):
 
     first(0)
     first(1)
-    for o in range(4):
-        second(0, o)
     first(2)
+    second(0, 0)
+    second(0, 1)
     first(3)
-    for o in range(4):
-        for i in (1, 2, 3):
-            second(i, o)
+    for i, o in ((0, 2), (0, 3), (1, 0), (2, 0), (1, 1), (1, 2), (1, 3), (3, 0), (2, 1), (3, 1), (2, 2), (3, 2), (2, 3), (3, 3)):
+        second(i, o)
 
     for o in range(4):
         cols = slice(C * o, C * o + C)

from concourse.bass import DstId, RemoteDMATransfer, IndirectOffsetOnAxis
from concourse.mybir import dt, AluOpType, ActivationFunctionType

N, C = 4, 512
W = 4 * C
BF, F8 = "bfloat16", "float8_e4m3fn_x4"
SCRATCH = {
    "lst": ("sbuf", [128, 4], "int32"),
    "tabs": ("sbuf", [128, 32], "int32"),
    "quad": ("sbuf", [128, 32], "int32"),
    "offs": ("sbuf", [128, 128], "uint16"),
    "w1b": ("sbuf", [128, 4096], BF), "xb": ("sbuf", [128, W], BF), "ab": ("sbuf", [128, W], BF),
    "w2g": ("sbuf", [128, W], BF), "bb": ("sbuf", [128, W], BF),
    "h0": ("sbuf", [128, W], BF), "h1": ("sbuf", [128, W], BF), "h2": ("sbuf", [128, W], BF), "h3": ("sbuf", [128, W], BF),
    "xq": ("sbuf", [128, C], F8), "xp": ("sbuf", [128, C], "uint8"),
    "aq": ("sbuf", [128, N * C], F8), "ap": ("sbuf", [128, N * C], "uint8"),
    "bq": ("sbuf", [128, N * C], F8), "bp": ("sbuf", [128, N * C], "uint8"),
    "hq": ("sbuf", [128, N * C], F8), "hp": ("sbuf", [128, N * C], "uint8"),
    "yb": ("sbuf", [128, W], "float32"),
    "zps": ("psum", [128, W], "float32"),
    "yps": ("psum", [128, W], "float32"),
}
SEMAPHORES = (["lact", "ltab", "lw1", "lx", "lxg", "vquad", "vrep", "voff", "gath0", "gath1", "qa0", "qa1", "qx", "qb",
               "bcs", "bcv", "sent", "stored"]
              + ["%s%d" % (k, i) for i in range(4) for k in ("ix", "z", "e", "h", "yd", "yc", "ax", "ay", "az", "bx", "by", "bz")])


def lanes(core, cores, topo):
    others = [c for c in cores if c != core]
    far = [c for c in others if topo.chip(c) != topo.chip(core)]
    near = [c for c in others if topo.chip(c) == topo.chip(core)]
    out = sorted({e for c in far for e in topo.engines(core, c)})
    plan = {}
    for group, es in ((far, out), (near, [e for c in near[:1] for e in topo.engines(core, c) if e not in out])):
        for i, c in enumerate(group):
            k = len(es) // len(group)
            plan[c] = es[i * k:i * k + k]
    return plan


def rank_program(g, core, T, topo):
    r = T.rank_of(core)
    if r is None:
        return
    S = T.sem
    MUL, ADD, MAX = AluOpType.mult, AluOpType.add, AluOpType.max
    COPY, RELU = ActivationFunctionType.Copy, ActivationFunctionType.Relu
    cores = list(T.cores)
    send = lanes(core, cores, topo)
    recv = {s: lanes(cores[s], cores, topo)[core] for s in range(N) if s != r}
    near = [s for s in recv if topo.chip(cores[s]) == topo.chip(core)]
    far = sorted([s for s in recv if s not in near], key=lambda s: topo.die(cores[s]) != topo.die(core))
    order = [r] + near + far

    def q(name, s, a=0, n=C):
        return T[name][:, C * s + a:C * s + a + n]

    def tab(eng, h, c):
        eng.dma_start(T.tabs[16 * h:16 * h + 16, 4 * c:4 * c + 4], T.act[16 * c:16 * c + 16, :]).then_inc(S.ltab, 16)

    XG = 256
    g.sync.dma_start(T.lst[:], T.act[:]).then_inc(S.lact, 16)
    for c in range(8):
        tab(g.sync, 0, c)
        tab(g.scalar, 1, c)
    g.scalar.dma_start(T.w1b[:], T.w1[:]).then_inc(S.lw1, 16)
    g.scalar.dma_start(T.xb[:, XG:], T.x[:, XG:]).then_inc(S.lx, 16)
    g.dma_start(T.xb[:, 0:XG], T.x[:, 0:XG]).then_inc(S.lxg, 16)

    total = [0]

    def fused(sem, pieces):
        tr = []
        for c in cores:
            if c == core:
                continue
            rid, pid, _ = topo.addr(c)
            n = len(send[c]) // len(pieces)
            for i, p in enumerate(pieces):
                tr.append(RemoteDMATransfer(dst_ids=[DstId(rid=rid, pnc=pid)], dma_engine_mask=sum(1 << e for e in send[c][i * n:i * n + n]),
                                            remote_sem=S["%s%d" % (sem, r)], src=p, dst=p))
                total[0] += n
        g.remote_dma_fused(tr, local_sem=S.sent)

    def codes(name, b, n=1):
        return q(name, r, 128 * b, 128 * n).bitcast(dt.uint8)

    g.wait_ge(S.lact, 16)
    for t in range(4):
        if t == 3:
            g.wait_ge(S.qa0, 1)
            fused("ax", [codes("aq", 0, 2)])
        g.indirect_dma_start(T.w2g[:, C * t:C * t + C], None, T.w2[:], IndirectOffsetOnAxis(ap=T.lst[:, t:t + 1], axis=0),
                             bounds_check=1023).then_inc(S["ix%d" % t], 16)
    g.wait_ge(S.qa1, 1)
    fused("ay", [q("ap", r), codes("aq", 2)])
    fused("az", [codes("aq", 3)])
    g.wait_ge(S.qb, 1)
    fused("bx", [q("bp", r), codes("bq", 0)])
    fused("by", [codes("bq", 1), codes("bq", 2)])
    fused("bz", [codes("bq", 3)])
    g.wait_ge(S.sent, total[0])

    v, a = g.vector, g.scalar
    v.wait_ge(S.ltab, 256)
    for b in range(4):
        v.tensor_scalar(T.quad[0:32, 8 * b:8 * b + 8], T.tabs[0:32, b:32:4], 4, None, MUL).then_inc(S.vquad, 1)
    v.wait_ge(S.vquad, 4)
    for k in range(1, 4):
        v.tensor_copy(T.quad[32 * k:32 * k + 32, :], T.quad[0:32, :]).then_inc(S.vrep, 1)
    v.wait_ge(S.vrep, 3)
    for t in range(4):
        v.tensor_scalar(T.offs[:, 32 * t:32 * t + 32], T.quad[:], t, None, ADD).then_inc(S.voff, 1)
    for e in (v, a):
        e.wait_ge(S.voff, 4)
        e.wait_ge(S.lw1, 16)
    for k, (lo, hi) in enumerate(((0, 256), (256, 512))):

        def gather(t):
            return (T.ab[:, 4 * lo + t:4 * hi:4],
                    T.w1b[:, 0:4096].indirect(T.offs[:, 32 * t + lo // 16:32 * t + hi // 16]))

        for t in (0, 1):
            v.tensor_copy(*gather(t)).then_inc(S["gath%d" % k], 1)
        for t in (2, 3):
            a.activation(*gather(t), COPY).then_inc(S["gath%d" % k], 1)
        v.wait_ge(S["gath%d" % k], 4)
        v.quantize_mx(q("aq", r, lo, hi - lo), q("ap", r, lo, hi - lo), T.ab[:, 4 * lo:4 * hi]).then_inc(S["qa%d" % k], 1)
    v.wait_ge(S.lx, 16)
    v.wait_ge(S.lxg, 16)
    v.quantize_mx(T.xq[:], T.xp[:], T.xb[:]).then_inc(S.qx, 1)

    def relu(i, b, vec):
        e = v if vec else a
        out, z = T["h%d" % order[i]][:, b:W:4], T.zps[:, C * b:C * b + C]
        e.wait_ge(S["z%d" % b], i + 1)
        if vec:
            v.tensor_scalar(out, z, 0.0, 0.05, MAX, MUL).then_inc(S["e%d" % b], 1)
        else:
            a.activation(out, z, RELU, scale=0.05).then_inc(S["e%d" % b], 1)

    def hidden(i, scal, vect):
        s = order[i]
        for b in scal:
            relu(i, b, False)
        for b in vect:
            relu(i, b, True)
        for b in range(4):
            v.wait_ge(S["e%d" % b], i + 1)
        v.quantize_mx(q("hq", s), q("hp", s), T["h%d" % s][:]).then_inc(S["h%d" % s], 1)

    def rows(t):
        return T.bb[:, t:W:4], T.w2g[:, C * t:C * t + C]

    for t in (0, 1):
        a.wait_ge(S["ix%d" % t], 16)
        a.activation(*rows(t), COPY).then_inc(S.bcs, 1)
    hidden(0, (0, 2), (1, 3))
    a.wait_ge(S.ix2, 16)
    a.activation(*rows(2), COPY).then_inc(S.bcs, 1)
    v.wait_ge(S.ix3, 16)
    v.tensor_copy(*rows(3)).then_inc(S.bcv, 1)
    v.wait_ge(S.bcv, 1)
    v.wait_ge(S.bcs, 3)
    v.quantize_mx(q("bq", r), q("bp", r), T.bb[:]).then_inc(S.qb, 1)
    hidden(1, (0, 1, 2), (3,))
    hidden(2, (0, 2), (1, 3))
    hidden(3, (0, 1, 2), (3,))
    for o in range(4):
        cols = slice(C * o, C * o + C)
        (a if o % 2 else v).wait_ge(S["yd%d" % o], 1)
        if o % 2 == 0:
            v.tensor_copy(T.yb[:, cols], T.yps[:, cols]).then_inc(S["yc%d" % o], 1)
        else:
            a.activation(T.yb[:, cols], T.yps[:, cols], COPY).then_inc(S["yc%d" % o], 1)

    p = g.tensor

    def first(i):
        s = order[i]
        for k in ("qa0", "qa1", "qx") if s == r else ():
            p.wait_ge(S[k], 1)
        for k in ("ax", "ay") if s != r else ():
            p.wait_ge(S["%s%d" % (k, s)], len(recv[s]))
        for b in range(4):
            if s != r and b == 3:
                p.wait_ge(S["az%d" % s], len(recv[s]))
            if i:
                p.wait_ge(S["e%d" % b], i)
            p.matmul_mx(T.zps[:, C * b:C * b + C], q("aq", s, 128 * b, 128), q("ap", s, 128 * b, 128), T.xq[:], T.xp[:],
                        True, True).then_inc(S["z%d" % b], 1)

    def second(i, o):
        s = order[i]
        if o == 0:
            p.wait_ge(S["h%d" % s], 1)
        if s == r:
            if o == 0:
                p.wait_ge(S.qb, 1)
        elif o != 2:
            p.wait_ge(S["%s%d" % (("bx", "by", None, "bz")[o], s)], len(recv[s]))
        m = p.matmul_mx(T.yps[:, C * o:C * o + C], q("bq", s, 128 * o, 128), q("bp", s, 128 * o, 128), q("hq", s), q("hp", s),
                        i == 0, i == N - 1)
        if i == N - 1:
            m.then_inc(S["yd%d" % o], 1)

    first(0)
    first(1)
    first(2)
    second(0, 0)
    second(0, 1)
    first(3)
    for i, o in ((0, 2), (0, 3), (1, 0), (2, 0), (1, 1), (1, 2), (1, 3), (3, 0), (2, 1), (3, 1), (2, 2), (3, 2), (2, 3), (3, 3)):
        second(i, o)

    for o in range(4):
        cols = slice(C * o, C * o + C)
        g.sync.wait_ge(S["yc%d" % o], 1)
        g.sync.dma_start(T.y[:, cols], T.yb[:, cols]).then_inc(S.stored, 16)
    g.sync.wait_ge(S.stored, 64)
